import numpy as np
import ml_dtypes


def mxq(x, axis, fmt="e4m3"):
    dtype, down = {"e4m3": (ml_dtypes.float8_e4m3fn, 7), "e5m2": (ml_dtypes.float8_e5m2, 14)}[fmt]
    v = np.moveaxis(np.asarray(x, np.float32).astype(ml_dtypes.bfloat16).astype(np.float64), axis, -1)
    blocks = v.reshape(v.shape[:-1] + (-1, 32))
    amax = np.abs(blocks).max(-1, keepdims=True)
    byte = np.maximum(np.where(amax > 0, np.frexp(amax)[1] - 1 + 127, 0) - down, 1)
    scale = np.exp2(byte - 127.0)
    codes = (blocks / scale).astype(np.float32).astype(dtype).astype(np.float64)
    return np.moveaxis((codes * scale).reshape(v.shape), -1, axis)


WIDE = False


def mx_kscale(k, group=512):
    if not WIDE:
        return np.ones(k)
    levels = np.array([18, -18])
    if group != 512:
        return np.exp2(np.random.permutation(np.resize(levels, k // group))).repeat(group)
    if k % 512:
        return np.exp2(np.random.permutation(np.resize(levels, k // 32))).repeat(32)
    a = np.empty((k // 512, 16))
    for p in range(k // 512):
        a[p, :8] = np.random.permutation(np.resize(levels, 8))
        for g in range(8):
            far = levels[np.abs(levels - a[p, g]) >= 10]
            a[p, g + 8] = far[np.random.randint(len(far))]
    return np.exp2(a.ravel()).repeat(32)


def f64(x):
    return np.asarray(x).astype(np.float64)


def sigmoid(v):
    return 1.0 / (1.0 + np.exp(-v))


G, D, M, O, N = 4, 128, 128, 128, 512


def setup_inputs():
    n = np.random.standard_normal
    s_d = mx_kscale(D, 0)
    s_o = mx_kscale(O, 0)
    return {
        "x": (n((G, D, N)) * s_d[:, None]).astype(np.float32),
        "w1": (n((G, D, M)) / np.sqrt(D) / s_d[:, None]).astype(np.float32),
        "w2": (n((G, D, M)) / np.sqrt(D) / s_d[:, None]).astype(np.float32),
        "w3": (n((G, D, M)) / np.sqrt(D) / s_d[:, None]).astype(np.float32),
        "wo": (n((G, O, M)) / np.sqrt(O) / s_o[:, None]).astype(np.float32),
        "dy": (n((G, O, N)) * s_o[:, None]).astype(np.float32),
        "old": (0.3 * n((G, M, N))).astype(np.float32),
    }


def reference(x, w1, w2, w3, wo, dy, old):
    w1q = mxq(f64(w1), 1, "e4m3")
    xq = mxq(f64(x), 1, "e4m3")
    z1 = w1q.transpose(0, 2, 1) @ xq
    w2q = mxq(f64(w2), 1, "e4m3")
    z2 = w2q.transpose(0, 2, 1) @ xq
    w3q = mxq(f64(w3), 1, "e4m3")
    z3 = w3q.transpose(0, 2, 1) @ xq
    sg = sigmoid(z1 * z2 + z3)
    woq = mxq(f64(wo), 1, "e4m3")
    dyq = mxq(f64(dy), 1, "e4m3")
    c0 = woq.transpose(0, 2, 1) @ dyq
    dsg = c0 * np.tanh(z3)
    dz3 = c0 * sg * (1.0 - np.square(np.tanh(z3))) + dsg * sg * (1.0 - sg)
    y = dz3 + f64(old)
    return y

@@ -1,0 +1,226 @@
+from contextlib import ExitStack
+
+import concourse.mybir as mybir
+
+G, D, M, N = 4, 128, 128, 512
+FLOPS = 4 * 2 * G * D * M * N
+
+F32 = mybir.dt.float32
+BF16 = mybir.dt.bfloat16
+U32 = mybir.dt.uint32
+U8 = mybir.dt.uint8
+FP8X4 = mybir.dt.float8_e4m3fn_x4
+ALU = mybir.AluOpType
+ACT = mybir.ActivationFunctionType
+
+P = 128
+PACK = 4
+ROWS = 32
+HALF = 256
+NMM = 128
+
+
+def tile_rows_bbilinsig_kernel(tc, x, w1, w2, w3, wo, dy, old, out):
+    nc = tc.nc
+    with ExitStack() as ctx:
+        sb = ctx.enter_context(tc.tile_pool(name="sb", bufs=1))
+        ps = ctx.enter_context(tc.psum_pool(name="ps", bufs=1))
+        ctx.enter_context(tc.manual_schedule())
+
+        raw, packed, codes, scales = {}, {}, {}, {}
+
+        def load(name, src, cols):
+            width = cols.stop - cols.start
+            raw[name] = sb.tile([P, PACK, width], F32, name="raw_" + name)
+            packed[name] = sb.tile([P, width, PACK], BF16, name="packed_" + name, align_bytes=64)
+            codes[name] = sb.tile([P, width], U32, name="codes_" + name, align_bytes=64)
+            scales[name] = sb.tile([P, width], U8, name="scales_" + name, align_bytes=64)
+            nc.sync.dma_start(out=raw[name][:], in_=src.rearrange("g (p j) n -> (g p) j n", j=PACK)[:, :, cols])
+
+        def views(name, cols):
+            dst = packed[name][:, cols, :].rearrange("p (c i) j -> p c j i", i=4)
+            src = raw[name][:, :, cols].rearrange("p j (c i) -> p c j i", i=4)
+            return dst, src
+
+        def cast_v(name, cols=slice(None)):
+            dst, src = views(name, cols)
+            nc.vector.tensor_copy(out=dst, in_=src)
+
+        def cast_s(name, cols=slice(None)):
+            dst, src = views(name, cols)
+            nc.scalar.copy(out=dst, in_=src)
+
+        def quant(name):
+            nc.vector.quantize_mx(out=codes[name][:].bitcast(FP8X4), scales=scales[name][:],
+                                  in_=packed[name][:].rearrange("p n j -> p (n j)"))
+
+        bank_a = [ps.tile([P, 2, HALF], F32, name="bank_a%d" % g) for g in range(G)]
+        bank_b = [ps.tile([P, 2, HALF], F32, name="bank_b%d" % g) for g in range(G)]
+
+        def groups(k):
+            return (2 * (k % 2), 2 * (k % 2) + 1)
+
+        def product(k, wname, aname, bank, slot):
+            aname = aname + str(k // 2)
+            for c in range(HALF // NMM):
+                cols = slice(c * NMM, (c + 1) * NMM)
+                for g in groups(k):
+                    rows = slice(ROWS * g, ROWS * (g + 1))
+                    nc.tensor.matmul_mx(out=bank[g][:, slot, cols],
+                                        lhsT=codes[wname][rows, :].bitcast(FP8X4), lhsT_scale=scales[wname][rows, :],
+                                        rhs=codes[aname][rows, cols].bitcast(FP8X4), rhs_scale=scales[aname][rows, cols],
+                                        start=True, stop=True)
+
+        def mm_z1(k):
+            product(k, "w1", "x", bank_a, 0)
+
+        def mm_z3(k):
+            product(k, "w3", "x", bank_a, 1)
+
+        def mm_z2(k):
+            product(k, "w2", "x", bank_b, 0)
+
+        def mm_c0(k):
+            product(k, "wo", "dy", bank_b, 1)
+
+        val = {}
+        for nm in ("z1", "a", "u", "t", "sm", "n", "q", "r", "d", "o"):
+            for k in range(4):
+                val[nm, k] = sb.tile([P, 2, HALF], F32, name="%s%d" % (nm, k))
+
+        def s_z1(k):
+            for i, g in enumerate(groups(k)):
+                nc.scalar.copy(out=val["z1", k][:, i, :], in_=bank_a[g][:, 0, :])
+
+        def s_t(k):
+            for i, g in enumerate(groups(k)):
+                nc.scalar.activation(out=val["t", k][:, i, :], in_=bank_a[g][:, 1, :], func=ACT.Tanh)
+
+        def s_sm(k):
+            nc.scalar.activation(out=val["sm", k][:], in_=val["u", k][:], func=ACT.Sigmoid, scale=-1.0)
+
+        def v_a(k):
+            for i, g in enumerate(groups(k)):
+                nc.vector.tensor_tensor(out=val["a", k][:, i, :], in0=val["z1", k][:, i, :], in1=bank_b[g][:, 0, :], op=ALU.mult)
+
+        def v_u(k):
+            for i, g in enumerate(groups(k)):
+                nc.vector.tensor_tensor(out=val["u", k][:, i, :], in0=val["a", k][:, i, :], in1=bank_a[g][:, 1, :], op=ALU.add)
+
+        def v_n(k):
+            for i, g in enumerate(groups(k)):
+                nc.vector.scalar_tensor_tensor(out=val["n", k][:, i, :], in0=val["sm", k][:, i, :], scalar=-1.0,
+                                               in1=bank_b[g][:, 1, :], op0=ALU.add, op1=ALU.mult)
+
+        def e_q(k, eng):
+            eng.tensor_tensor(out=val["q", k][:], in0=val["t", k][:], in1=val["sm", k][:], op=ALU.subtract)
+
+        def e_r(k, eng):
+            eng.tensor_tensor(out=val["r", k][:], in0=val["q", k][:], in1=val["t", k][:], op=ALU.mult)
+
+        def v_d(k, part=slice(0, 2)):
+            nc.vector.scalar_tensor_tensor(out=val["d", k][:, part, :], in0=val["r", k][:, part, :], scalar=-1.0,
+                                           in1=val["n", k][:, part, :], op0=ALU.add, op1=ALU.mult)
+
+        def e_o(k, eng, part=slice(0, 2)):
+            cols = slice(HALF * (k // 2), HALF * (k // 2 + 1))
+            eng.tensor_tensor(out=val["o", k][:, part, :], in0=val["d", k][:, part, :],
+                              in1=olds[k % 2][:, part, cols], op=ALU.add)
+            g0 = 2 * (k % 2)
+            nc.sync.dma_start(out=out[g0 + part.start : g0 + part.stop, :, cols].rearrange("g m n -> m g n"),
+                              in_=val["o", k][:, part, :])
+
+        first, second, whole = slice(0, HALF), slice(HALF, N), slice(0, M)
+        load("x0", x, first)
+        load("w1", w1, whole)
+        load("w2", w2, whole)
+        load("w3", w3, whole)
+        load("wo", wo, whole)
+        load("dy0", dy, first)
+        load("x1", x, second)
+        load("dy1", dy, second)
+        olds = []
+        for i in range(2):
+            olds.append(sb.tile([P, 2, N], F32, name="old%d" % i))
+            nc.sync.dma_start(out=olds[i][:], in_=old[2 * i : 2 * i + 2].rearrange("g m n -> m g n"))
+
+        warm_in = sb.tile([P, 1], F32, name="warm_in")
+        warm_out = sb.tile([P, 1], F32, name="warm_out")
+        nc.vector.memset(warm_in[:], 0.0)
+        nc.scalar.activation(out=warm_out[:], in_=warm_in[:], func=ACT.Sigmoid)
+
+        cast_v("x0")
+        cast_s("w1")
+        quant("x0")
+        cast_v("w2")
+        quant("w1")
+        quant("w2")
+        mm_z1(0)
+        mm_z2(0)
+        mm_z1(1)
+        cast_v("w3")
+        quant("w3")
+        s_z1(0)
+        mm_z3(0)
+        mm_z2(1)
+        s_t(0)
+        v_a(0)
+        v_u(0)
+        s_z1(1)
+        mm_z3(1)
+        s_sm(0)
+        s_t(1)
+        cast_v("wo")
+        cast_v("dy0")
+        quant("wo")
+        e_q(0, nc.gpsimd)
+        v_a(1)
+        v_u(1)
+        cast_s("x1", slice(0, 128))
+        s_sm(1)
+        cast_s("x1", slice(128, 256))
+        quant("dy0")
+        mm_c0(0)
+        mm_c0(1)
+        e_r(0, nc.vector)
+        e_q(1, nc.gpsimd)
+        v_n(0)
+        v_n(1)
+        cast_s("dy1")
+        quant("x1")
+        mm_z1(2)
+        mm_z2(2)
+        mm_z1(3)
+        s_z1(2)
+        mm_z3(2)
+        mm_z2(3)
+        v_d(0)
+        e_r(1, nc.vector)
+        s_t(2)
+        e_o(0, nc.gpsimd)
+        v_a(2)
+        v_u(2)
+        s_z1(3)
+        mm_z3(3)
+        s_t(3)
+        s_sm(2)
+        v_d(1)
+        e_o(1, nc.gpsimd)
+        v_a(3)
+        v_u(3)
+        s_sm(3)
+        e_q(2, nc.vector)
+        quant("dy1")
+        mm_c0(2)
+        mm_c0(3)
+        e_r(2, nc.vector)
+        e_q(3, nc.gpsimd)
+        v_n(2)
+        v_n(3)
+        v_d(2)
+        e_r(3, nc.vector)
+        e_o(2, nc.vector)
+        v_d(3, slice(0, 1))
+        v_d(3, slice(1, 2))
+        e_o(3, nc.vector, slice(0, 1))
+        e_o(3, nc.vector, slice(1, 2))

@@ -50,6 +50,10 @@ def tile_rows_bbilinsig_kernel(tc, x, w1, w2, w3, wo, dy, old, out):
             dst, src = views(name, cols)
             nc.scalar.copy(out=dst, in_=src)
 
+        def cast_g(name, cols=slice(None)):
+            nc.gpsimd.tensor_scalar(out=packed[name][:, cols, :], in0=raw[name][:, :, cols].rearrange("p j n -> p n j"),
+                                    scalar1=1.0, scalar2=0.0, op0=ALU.mult, op1=ALU.add)
+
         def quant(name):
             nc.vector.quantize_mx(out=codes[name][:].bitcast(FP8X4), scales=scales[name][:],
                                   in_=packed[name][:].rearrange("p n j -> p (n j)"))
@@ -92,12 +96,13 @@ def tile_rows_bbilinsig_kernel(tc, x, w1, w2, w3, wo, dy, old, out):
             for i, g in enumerate(groups(k)):
                 nc.scalar.copy(out=val["z1", k][:, i, :], in_=bank_a[g][:, 0, :])
 
-        def s_t(k):
-            for i, g in enumerate(groups(k)):
+        def s_t(k, part=slice(0, 2)):
+            for i in range(part.start, part.stop):
+                g = groups(k)[i]
                 nc.scalar.activation(out=val["t", k][:, i, :], in_=bank_a[g][:, 1, :], func=ACT.Tanh)
 
-        def s_sm(k):
-            nc.scalar.activation(out=val["sm", k][:], in_=val["u", k][:], func=ACT.Sigmoid, scale=-1.0)
+        def s_sm(k, part=slice(0, 2)):
+            nc.scalar.activation(out=val["sm", k][:, part, :], in_=val["u", k][:, part, :], func=ACT.Sigmoid, scale=-1.0)
 
         def v_a(k):
             for i, g in enumerate(groups(k)):
@@ -149,78 +154,83 @@ def tile_rows_bbilinsig_kernel(tc, x, w1, w2, w3, wo, dy, old, out):
         nc.vector.memset(warm_in[:], 0.0)
         nc.scalar.activation(out=warm_out[:], in_=warm_in[:], func=ACT.Sigmoid)
 
-        cast_v("x0")
-        cast_s("w1")
+        cast_v("x0", slice(0, 160))
+        cast_s("x0", slice(160, 256))
+        cast_v("w1")
         quant("x0")
-        cast_v("w2")
         quant("w1")
-        quant("w2")
         mm_z1(0)
-        mm_z2(0)
         mm_z1(1)
-        cast_v("w3")
-        quant("w3")
         s_z1(0)
+        s_z1(1)
+        cast_v("w2")
+        cast_v("w3")
+        quant("w2")
+        quant("w3")
+        mm_z2(0)
         mm_z3(0)
         mm_z2(1)
-        s_t(0)
+        mm_z3(1)
+        cast_v("wo")
+        quant("wo")
+        cast_g("dy0", slice(0, 128))
+        cast_s("dy0", slice(128, 256))
         v_a(0)
         v_u(0)
-        s_z1(1)
-        mm_z3(1)
+        s_t(0, slice(0, 1))
         s_sm(0)
-        s_t(1)
-        cast_v("wo")
-        cast_v("dy0")
-        quant("wo")
-        e_q(0, nc.gpsimd)
+        s_t(0, slice(1, 2))
         v_a(1)
         v_u(1)
-        cast_s("x1", slice(0, 128))
+        s_t(1, slice(0, 1))
         s_sm(1)
+        s_t(1, slice(1, 2))
         cast_s("x1", slice(128, 256))
         quant("dy0")
         mm_c0(0)
         mm_c0(1)
-        e_r(0, nc.vector)
-        e_q(1, nc.gpsimd)
+        e_q(0, nc.vector)
+        cast_v("x1", slice(0, 128))
+        e_r(0, nc.gpsimd)
         v_n(0)
         v_n(1)
-        cast_s("dy1")
         quant("x1")
         mm_z1(2)
+        mm_z3(2)
         mm_z2(2)
         mm_z1(3)
-        s_z1(2)
-        mm_z3(2)
+        mm_z3(3)
         mm_z2(3)
+        cast_s("dy1")
+        s_z1(2)
+        s_t(2)
+        s_z1(3)
+        s_t(3)
+        e_q(1, nc.vector)
         v_d(0)
         e_r(1, nc.vector)
-        s_t(2)
         e_o(0, nc.gpsimd)
         v_a(2)
         v_u(2)
-        s_z1(3)
-        mm_z3(3)
-        s_t(3)
         s_sm(2)
         v_d(1)
-        e_o(1, nc.gpsimd)
-        v_a(3)
-        v_u(3)
-        s_sm(3)
-        e_q(2, nc.vector)
         quant("dy1")
         mm_c0(2)
+        e_o(1, nc.gpsimd)
+        v_a(3)
         mm_c0(3)
-        e_r(2, nc.vector)
-        e_q(3, nc.gpsimd)
+        v_u(3)
+        s_sm(3, slice(0, 1))
+        s_sm(3, slice(1, 2))
+        e_q(2, nc.vector)
+        e_q(3, nc.vector)
+        e_r(2, nc.gpsimd)
         v_n(2)
         v_n(3)
-        v_d(2)
         e_r(3, nc.vector)
-        e_o(2, nc.vector)
+        v_d(2)
         v_d(3, slice(0, 1))
+        e_o(2, nc.vector)
         v_d(3, slice(1, 2))
         e_o(3, nc.vector, slice(0, 1))
         e_o(3, nc.vector, slice(1, 2))

from contextlib import ExitStack

import concourse.mybir as mybir

G, D, M, N = 4, 128, 128, 512
FLOPS = 4 * 2 * G * D * M * N

F32 = mybir.dt.float32
BF16 = mybir.dt.bfloat16
U32 = mybir.dt.uint32
U8 = mybir.dt.uint8
FP8X4 = mybir.dt.float8_e4m3fn_x4
ALU = mybir.AluOpType
ACT = mybir.ActivationFunctionType

P = 128
PACK = 4
ROWS = 32
HALF = 256
NMM = 128


def tile_rows_bbilinsig_kernel(tc, x, w1, w2, w3, wo, dy, old, out):
    nc = tc.nc
    with ExitStack() as ctx:
        sb = ctx.enter_context(tc.tile_pool(name="sb", bufs=1))
        ps = ctx.enter_context(tc.psum_pool(name="ps", bufs=1))
        ctx.enter_context(tc.manual_schedule())

        raw, packed, codes, scales = {}, {}, {}, {}

        def load(name, src, cols):
            width = cols.stop - cols.start
            raw[name] = sb.tile([P, PACK, width], F32, name="raw_" + name)
            packed[name] = sb.tile([P, width, PACK], BF16, name="packed_" + name, align_bytes=64)
            codes[name] = sb.tile([P, width], U32, name="codes_" + name, align_bytes=64)
            scales[name] = sb.tile([P, width], U8, name="scales_" + name, align_bytes=64)
            nc.sync.dma_start(out=raw[name][:], in_=src.rearrange("g (p j) n -> (g p) j n", j=PACK)[:, :, cols])

        def views(name, cols):
            dst = packed[name][:, cols, :].rearrange("p (c i) j -> p c j i", i=4)
            src = raw[name][:, :, cols].rearrange("p j (c i) -> p c j i", i=4)
            return dst, src

        def cast_v(name, cols=slice(None)):
            dst, src = views(name, cols)
            nc.vector.tensor_copy(out=dst, in_=src)

        def cast_s(name, cols=slice(None)):
            dst, src = views(name, cols)
            nc.scalar.copy(out=dst, in_=src)

        def cast_g(name, cols=slice(None)):
            nc.gpsimd.tensor_scalar(out=packed[name][:, cols, :], in0=raw[name][:, :, cols].rearrange("p j n -> p n j"),
                                    scalar1=1.0, scalar2=0.0, op0=ALU.mult, op1=ALU.add)

        def quant(name):
            nc.vector.quantize_mx(out=codes[name][:].bitcast(FP8X4), scales=scales[name][:],
                                  in_=packed[name][:].rearrange("p n j -> p (n j)"))

        bank_a = [ps.tile([P, 2, HALF], F32, name="bank_a%d" % g) for g in range(G)]
        bank_b = [ps.tile([P, 2, HALF], F32, name="bank_b%d" % g) for g in range(G)]

        def groups(k):
            return (2 * (k % 2), 2 * (k % 2) + 1)

        def product(k, wname, aname, bank, slot):
            aname = aname + str(k // 2)
            for c in range(HALF // NMM):
                cols = slice(c * NMM, (c + 1) * NMM)
                for g in groups(k):
                    rows = slice(ROWS * g, ROWS * (g + 1))
                    nc.tensor.matmul_mx(out=bank[g][:, slot, cols],
                                        lhsT=codes[wname][rows, :].bitcast(FP8X4), lhsT_scale=scales[wname][rows, :],
                                        rhs=codes[aname][rows, cols].bitcast(FP8X4), rhs_scale=scales[aname][rows, cols],
                                        start=True, stop=True)

        def mm_z1(k):
            product(k, "w1", "x", bank_a, 0)

        def mm_z3(k):
            product(k, "w3", "x", bank_a, 1)

        def mm_z2(k):
            product(k, "w2", "x", bank_b, 0)

        def mm_c0(k):
            product(k, "wo", "dy", bank_b, 1)

        val = {}
        for nm in ("z1", "a", "u", "t", "sm", "n", "q", "r", "d", "o"):
            for k in range(4):
                val[nm, k] = sb.tile([P, 2, HALF], F32, name="%s%d" % (nm, k))

        def s_z1(k):
            for i, g in enumerate(groups(k)):
                nc.scalar.copy(out=val["z1", k][:, i, :], in_=bank_a[g][:, 0, :])

        def s_t(k, part=slice(0, 2)):
            for i in range(part.start, part.stop):
                g = groups(k)[i]
                nc.scalar.activation(out=val["t", k][:, i, :], in_=bank_a[g][:, 1, :], func=ACT.Tanh)

        def s_sm(k, part=slice(0, 2)):
            nc.scalar.activation(out=val["sm", k][:, part, :], in_=val["u", k][:, part, :], func=ACT.Sigmoid, scale=-1.0)

        def v_a(k):
            for i, g in enumerate(groups(k)):
                nc.vector.tensor_tensor(out=val["a", k][:, i, :], in0=val["z1", k][:, i, :], in1=bank_b[g][:, 0, :], op=ALU.mult)

        def v_u(k):
            for i, g in enumerate(groups(k)):
                nc.vector.tensor_tensor(out=val["u", k][:, i, :], in0=val["a", k][:, i, :], in1=bank_a[g][:, 1, :], op=ALU.add)

        def v_n(k):
            for i, g in enumerate(groups(k)):
                nc.vector.scalar_tensor_tensor(out=val["n", k][:, i, :], in0=val["sm", k][:, i, :], scalar=-1.0,
                                               in1=bank_b[g][:, 1, :], op0=ALU.add, op1=ALU.mult)

        def e_q(k, eng):
            eng.tensor_tensor(out=val["q", k][:], in0=val["t", k][:], in1=val["sm", k][:], op=ALU.subtract)

        def e_r(k, eng):
            eng.tensor_tensor(out=val["r", k][:], in0=val["q", k][:], in1=val["t", k][:], op=ALU.mult)

        def v_d(k, part=slice(0, 2)):
            nc.vector.scalar_tensor_tensor(out=val["d", k][:, part, :], in0=val["r", k][:, part, :], scalar=-1.0,
                                           in1=val["n", k][:, part, :], op0=ALU.add, op1=ALU.mult)

        def e_o(k, eng, part=slice(0, 2)):
            cols = slice(HALF * (k // 2), HALF * (k // 2 + 1))
            eng.tensor_tensor(out=val["o", k][:, part, :], in0=val["d", k][:, part, :],
                              in1=olds[k % 2][:, part, cols], op=ALU.add)
            g0 = 2 * (k % 2)
            nc.sync.dma_start(out=out[g0 + part.start : g0 + part.stop, :, cols].rearrange("g m n -> m g n"),
                              in_=val["o", k][:, part, :])

        first, second, whole = slice(0, HALF), slice(HALF, N), slice(0, M)
        load("x0", x, first)
        load("w1", w1, whole)
        load("w2", w2, whole)
        load("w3", w3, whole)
        load("wo", wo, whole)
        load("dy0", dy, first)
        load("x1", x, second)
        load("dy1", dy, second)
        olds = []
        for i in range(2):
            olds.append(sb.tile([P, 2, N], F32, name="old%d" % i))
            nc.sync.dma_start(out=olds[i][:], in_=old[2 * i : 2 * i + 2].rearrange("g m n -> m g n"))

        warm_in = sb.tile([P, 1], F32, name="warm_in")
        warm_out = sb.tile([P, 1], F32, name="warm_out")
        nc.vector.memset(warm_in[:], 0.0)
        nc.scalar.activation(out=warm_out[:], in_=warm_in[:], func=ACT.Sigmoid)

        cast_v("x0", slice(0, 160))
        cast_s("x0", slice(160, 256))
        cast_v("w1")
        quant("x0")
        quant("w1")
        mm_z1(0)
        mm_z1(1)
        s_z1(0)
        s_z1(1)
        cast_v("w2")
        cast_v("w3")
        quant("w2")
        quant("w3")
        mm_z2(0)
        mm_z3(0)
        mm_z2(1)
        mm_z3(1)
        cast_v("wo")
        quant("wo")
        cast_g("dy0", slice(0, 128))
        cast_s("dy0", slice(128, 256))
        v_a(0)
        v_u(0)
        s_t(0, slice(0, 1))
        s_sm(0)
        s_t(0, slice(1, 2))
        v_a(1)
        v_u(1)
        s_t(1, slice(0, 1))
        s_sm(1)
        s_t(1, slice(1, 2))
        cast_s("x1", slice(128, 256))
        quant("dy0")
        mm_c0(0)
        mm_c0(1)
        e_q(0, nc.vector)
        cast_v("x1", slice(0, 128))
        e_r(0, nc.gpsimd)
        v_n(0)
        v_n(1)
        quant("x1")
        mm_z1(2)
        mm_z3(2)
        mm_z2(2)
        mm_z1(3)
        mm_z3(3)
        mm_z2(3)
        cast_s("dy1")
        s_z1(2)
        s_t(2)
        s_z1(3)
        s_t(3)
        e_q(1, nc.vector)
        v_d(0)
        e_r(1, nc.vector)
        e_o(0, nc.gpsimd)
        v_a(2)
        v_u(2)
        s_sm(2)
        v_d(1)
        quant("dy1")
        mm_c0(2)
        e_o(1, nc.gpsimd)
        v_a(3)
        mm_c0(3)
        v_u(3)
        s_sm(3, slice(0, 1))
        s_sm(3, slice(1, 2))
        e_q(2, nc.vector)
        e_q(3, nc.vector)
        e_r(2, nc.gpsimd)
        v_n(2)
        v_n(3)
        e_r(3, nc.vector)
        v_d(2)
        v_d(3, slice(0, 1))
        e_o(2, nc.vector)
        v_d(3, slice(1, 2))
        e_o(3, nc.vector, slice(0, 1))
        e_o(3, nc.vector, slice(1, 2))
